import numpy as np
import ml_dtypes


def mxq(x, axis, fmt="e4m3"):
    dtype, down = {"e4m3": (ml_dtypes.float8_e4m3fn, 7), "e5m2": (ml_dtypes.float8_e5m2, 14)}[fmt]
    v = np.moveaxis(np.asarray(x, np.float32).astype(ml_dtypes.bfloat16).astype(np.float64), axis, -1)
    blocks = v.reshape(v.shape[:-1] + (-1, 32))
    amax = np.abs(blocks).max(-1, keepdims=True)
    byte = np.maximum(np.where(amax > 0, np.frexp(amax)[1] - 1 + 127, 0) - down, 1)
    scale = np.exp2(byte - 127.0)
    codes = (blocks / scale).astype(np.float32).astype(dtype).astype(np.float64)
    return np.moveaxis((codes * scale).reshape(v.shape), -1, axis)


WIDE = False


def mx_kscale(k):
    if not WIDE:
        return np.ones(k)
    levels = np.array([10, -10, 5, -5, 0])
    if k % 512:
        return np.exp2(np.random.permutation(np.resize(levels, k // 32))).repeat(32)
    a = np.empty((k // 512, 16))
    for p in range(k // 512):
        a[p, :8] = np.random.permutation(np.resize(levels, 8))
        for g in range(8):
            far = levels[np.abs(levels - a[p, g]) >= 10]
            a[p, g + 8] = far[np.random.randint(len(far))]
    return np.exp2(a.ravel()).repeat(32)


def f64(x):
    return np.asarray(x).astype(np.float64)


def striped(idx):
    return np.tile(idx.reshape(-1, 16).T, (8, 1)).astype(np.uint16)


def unstriped(offs):
    return offs[:16].T.reshape(-1).astype(np.int64)


E2M1 = np.array([0.0, 0.5, 1.0, 1.5, 2.0, 3.0, 4.0, 6.0, -0.0, -0.5, -1.0, -1.5, -2.0, -3.0, -4.0, -6.0])


def pack_weight(w, fmt):
    k, n = w.shape
    w = f64(np.asarray(w, np.float32).astype(ml_dtypes.bfloat16)).reshape(k // 32, 32, n)
    amax = np.abs(w).max(1)
    if fmt == "e4m3":
        byte = np.frexp(amax)[1] - 1 + 127 - 7
    else:
        mant, ex = np.frexp(amax / 6.0)
        byte = np.where(mant > 0.5, ex, ex - 1) + 127
    byte = np.clip(np.where(amax > 0, byte, 1), 1, 254)
    scaled = (w * np.exp2(127.0 - byte)[:, None, :]).reshape(k, n).astype(np.float32)
    by_word = np.ascontiguousarray(scaled.reshape(k // 512, 128, 4, n).transpose(0, 1, 3, 2))
    if fmt == "e4m3":
        words = by_word.astype(ml_dtypes.float8_e4m3fn).view(np.uint8)
    else:
        c = by_word.astype(ml_dtypes.float4_e2m1fn).view(np.uint8) & 0xF
        words = (c[..., 0::2] | (c[..., 1::2] << 4)).reshape(k // 512, 128, 2 * n)
    return np.ascontiguousarray(words), np.ascontiguousarray(byte.astype(np.uint8).reshape(k // 512, 16, n))


def unpack_weight(words, scales, fmt):
    g, _, n = scales.shape
    words = np.ascontiguousarray(words).reshape(g, 128, n, -1)
    if fmt == "e4m3":
        vals = words.view(ml_dtypes.float8_e4m3fn).astype(np.float64)
    else:
        nib = np.empty((g, 128, n, 4), np.uint8)
        nib[..., 0::2] = words & 0xF
        nib[..., 1::2] = words >> 4
        vals = E2M1[nib]
    vals = vals * np.repeat(np.exp2(scales.astype(np.float64) - 127.0), 8, axis=1)[..., None]
    return vals.transpose(0, 1, 3, 2).reshape(g * 512, n)


def planes(y):
    n, m = y.shape
    v = y.astype(np.float32).astype(ml_dtypes.bfloat16).astype(np.float64).reshape(n // 32, 32, m)
    top = np.abs(v).max(1)
    byte = np.clip(np.where(top > 0, np.frexp(top)[1] - 1 + 127 - 7, 1), 1, 254)
    codes = (v * np.exp2(127.0 - byte)[:, None, :]).reshape(n, m).astype(np.float32).astype(ml_dtypes.float8_e4m3fn).view(np.uint8)
    words = codes.reshape(n // 512, 128, 4, m).transpose(0, 1, 3, 2)
    return np.ascontiguousarray(words), np.ascontiguousarray(byte.astype(np.uint8).reshape(n // 512, 16, m))


def d_silu(v):
    s = 1.0 / (1.0 + np.exp(-np.maximum(v, -700.0)))
    return s * (1.0 + v * (1.0 - s))


K, T, E, C, H, N = 512, 512, 4, 256, 512, 1536


def by_expert(wq, xq):
    return np.concatenate([wq[e].T @ xq[:, e * C:(e + 1) * C] for e in range(E)], axis=1)


def setup_inputs():
    n = np.random.standard_normal
    v = mx_kscale(N)
    u = mx_kscale(H)
    first = np.random.permutation(np.repeat(np.arange(E), T // E))
    second = (first + 1 + np.random.permutation(np.repeat(np.arange(E - 1), -(-T // (E - 1)))[:T])) % E
    while np.bincount(second, minlength=E).max() != T // E:
        load = np.bincount(second, minlength=E); hi, lo = int(load.argmax()), int(load.argmin())
        t = np.flatnonzero((second == hi) & (first != lo))[0]; second[t] = lo
    slot_token = np.empty(E * C, np.int64); pos = np.empty((2, T), np.int64); fill = np.zeros(E, np.int64)
    place = np.stack([np.random.permutation(C) for _ in range(E)])
    for r, deal in enumerate((first, second)):
        for t in np.random.permutation(T):
            e = deal[t]; j = e * C + place[e, fill[e]]; fill[e] += 1; slot_token[j] = t; pos[r, t] = j
    g = np.random.uniform(0.2, 0.8, T)
    dy = pack_weight(n((N, T)) * v[:, None], "e4m3")
    w2t = [pack_weight(m, "e4m3") for m in n((E, N, H)) / np.sqrt(N) / v[None, :, None] * u]
    w1t = pack_weight(n((H, K)) / np.sqrt(H) / u[:, None], "e2m1")
    return {
        "dy_words": dy[0],
        "dy_scales": dy[1],
        "w2t_words": np.stack([m[0] for m in w2t]),
        "w2t_scales": np.stack([m[1] for m in w2t]),
        "w1t_words": w1t[0],
        "w1t_scales": w1t[1],
        "a": (n((H, T))).astype(np.float32),
        "gate": np.stack([np.tile(g, (128, 1)), np.tile(1.0 - g, (128, 1))]).astype(np.float32),
        "offs": striped(slot_token),
        "pos1": striped(pos[0]),
        "pos2": striped(pos[1]),
    }


def reference(dy_words, dy_scales, w2t_words, w2t_scales, w1t_words, w1t_scales, a, gate, offs, pos1, pos2):
    w2t = np.stack([unpack_weight(w2t_words[e], w2t_scales[e], "e4m3") for e in range(E)])
    w1t = unpack_weight(w1t_words, w1t_scales, "e2m1")
    idx = unstriped(offs)
    gq = unpack_weight(dy_words, dy_scales, "e4m3")[:, idx]
    y = by_expert(w2t, gq)
    dh = sum(f64(gate[r, :1]) * y[:, unstriped(p)] for r, p in enumerate((pos1, pos2)))
    out_0 = w1t.T @ mxq(dh * d_silu(f64(a)), 0, "e4m3")
    return (out_0,) + planes(out_0)

@@ -1,0 +1,218 @@
+from contextlib import ExitStack
+
+import concourse.mybir as mybir
+from concourse.masks import make_identity
+
+K, T, E, C, H, N = 512, 512, 4, 256, 512, 1536
+FLOPS = 2 * (E * C * N * H + H * K * T)
+
+F32 = mybir.dt.float32
+BF16 = mybir.dt.bfloat16
+I32 = mybir.dt.int32
+U32 = mybir.dt.uint32
+U16 = mybir.dt.uint16
+U8 = mybir.dt.uint8
+FP8X4 = mybir.dt.float8_e4m3fn_x4
+FP4X4 = mybir.dt.float4_e2m1fn_x4
+ALU = mybir.AluOpType
+ACT = mybir.ActivationFunctionType
+
+P = 128
+PASSES = N // 512
+ROWS = H // P
+BLOCKS = T // P
+
+
+def tile_moe_sub_silu_kernel(
+    tc, dy_words, dy_scales, w2t_words, w2t_scales, w1t_words, w1t_scales, a, gate, offs, pos1, pos2,
+    out_0, out_1, out_2,
+):
+    nc = tc.nc
+    with ExitStack() as ctx:
+        sb = ctx.enter_context(tc.tile_pool(name="sb", bufs=1))
+        ps = ctx.enter_context(tc.psum_pool(name="ps", bufs=8))
+
+        def held(shape, dtype, name, tag=None):
+            return sb.tile(shape, dtype, name=name, tag=tag or name, align_bytes=64)
+
+        offs_t = sb.tile([P, E * C // 16], U16, name="offs_t")
+        pos_t = [sb.tile([P, T // 16], U16, name=f"pos_t{r}") for r in range(2)]
+
+        dy_sc = held([P, T], U8, "dy_sc")
+        w2_sc = held([P, E * PASSES, H], U8, "w2_sc")
+        w1_sc_raw = held([P, K], U8, "w1_sc_raw")
+        nc.vector.memset(dy_sc[:].bitcast(I32), 0)
+        nc.vector.memset(w2_sc[:].bitcast(I32), 0)
+        nc.vector.memset(w1_sc_raw[:].bitcast(I32), 0)
+
+        dy_w = held([P, PASSES, T], U32, "dy_w")
+        a_t = [held([P, 2, T], F32, f"a_t{h}") for h in range(2)]
+        w2_w = [held([P, PASSES, H], U32, f"w2_w{e}") for e in range(E)]
+        gate_t = held([P, 2, T], F32, "gate_t")
+        w1_raw = held([P, 2 * K], U8, "w1_raw")
+
+        nc.sync.dma_start(offs_t[:], offs)
+        a_rows = a.rearrange("(j p) t -> p j t", p=P)
+        nc.sync.dma_start(dy_w[:].bitcast(I32), dy_words.rearrange("s p t d -> p s (t d)").bitcast(I32))
+        for q in range(4):
+            nc.scalar.dma_start(
+                dy_sc[32 * q : 32 * q + 4 * PASSES, :].bitcast(I32), dy_scales[:, 4 * q : 4 * q + 4, :].bitcast(I32)
+            )
+        for h in range(2):
+            nc.sync.dma_start(a_t[h][:], a_rows[:, 2 * h : 2 * h + 2, :])
+        w2_sc_rows = w2t_scales.rearrange("e s (q r) i -> r q (e s) i", r=4)
+        for r in range(4):
+            nc.sync.dma_start(w2_sc[r:P:32, :, :].bitcast(I32), w2_sc_rows[r].bitcast(I32))
+        for e in range(E):
+            nc.sync.dma_start(
+                w2_w[e][:].bitcast(I32), w2t_words[e].rearrange("s p i d -> p s (i d)").bitcast(I32)
+            )
+        nc.sync.dma_start(pos_t[0][:], pos1)
+        nc.sync.dma_start(pos_t[1][:], pos2)
+        nc.sync.dma_start(gate_t[:], gate.rearrange("r p t -> p r t"))
+        nc.sync.dma_start(w1_raw[:].bitcast(I32), w1t_words[0].bitcast(I32))
+        w1_sc_rows = w1t_scales[0].rearrange("(q r) k -> r q k", r=4)
+        for r in range(4):
+            nc.sync.dma_start(w1_sc_raw[r:P:32, :].bitcast(I32), w1_sc_rows[r].bitcast(I32))
+
+        ident = held([P, P], F32, "ident")
+        make_identity(nc, ident[:])
+
+        silu_neg = held([P, BLOCKS, H], F32, "silu_neg")
+        sig = held([P, BLOCKS, H], F32, "sig")
+        a_turned = []
+        for j in range(ROWS):
+            bank = ps.tile([P, BLOCKS, P], F32, name="bank_a", tag="bank")
+            for b in range(BLOCKS):
+                nc.tensor.transpose(bank[:, b, :], a_t[j // 2][:, j % 2, b * P : (b + 1) * P], ident[:])
+            nc.scalar.activation(silu_neg[:, :, j * P : (j + 1) * P], bank[:], ACT.Silu, scale=-1.0)
+            a_turned.append(bank)
+
+        y = [held([P, E * C], F32, f"y{j}") for j in range(ROWS)]
+
+        def slots(e):
+            return offs_t[:, e * C // 16 : (e + 1) * C // 16]
+
+        g_w = [[held([P, C], U32, f"g_w{e}_{s}") for s in range(PASSES)] for e in range(E)]
+
+        def expert(e):
+            g_sc = held([P, C], U8, f"g_sc{e}")
+            nc.vector.tensor_copy(g_sc[:], dy_sc[:].indirect(slots(e)))
+            for s in range(PASSES):
+                nc.vector.tensor_copy(g_w[e][s][:], dy_w[:, s, :].indirect(slots(e)))
+            for half in range(ROWS // 2):
+                bank = ps.tile([P, 2, C], F32, name="bank_y", tag="bank")
+                for jj in range(2):
+                    cols = slice((2 * half + jj) * P, (2 * half + jj + 1) * P)
+                    for s in range(PASSES):
+                        nc.tensor.matmul_mx(
+                            out=bank[:, jj, :],
+                            lhsT=w2_w[e][:, s, cols].bitcast(FP8X4),
+                            lhsT_scale=w2_sc[:, e * PASSES + s, cols],
+                            rhs=g_w[e][s][:].bitcast(FP8X4),
+                            rhs_scale=g_sc[4 * s :, :],
+                            start=(s == 0),
+                            stop=(s == PASSES - 1),
+                        )
+                for jj in range(2):
+                    leave = nc.vector.tensor_copy if (e, half) == (E - 1, 1) else nc.scalar.copy
+                    leave(y[2 * half + jj][:, e * C : (e + 1) * C], bank[:, jj, :])
+
+        for j in range(ROWS):
+            nc.scalar.activation(sig[:, :, j * P : (j + 1) * P], a_turned[j][:], ACT.Sigmoid)
+        for e in range(E - 1):
+            expert(e)
+
+        neg_slope = [held([P, H], F32, f"neg_slope{b}") for b in range(BLOCKS)]
+        for b in range(BLOCKS):
+            nc.vector.scalar_tensor_tensor(
+                neg_slope[b][:], silu_neg[:, b, :], 1.0, sig[:, b, :], ALU.subtract, ALU.mult
+            )
+
+        expert(E - 1)
+
+        out_codes = held([P, T], U32, "out_codes")
+        out_sc = held([P, T], U8, "out_sc")
+        out_rows = out_0.rearrange("(p j) t -> p j t", j=4)
+        out_words = out_1[0].rearrange("p t d -> p (t d)").bitcast(I32)
+
+        def combine(b):
+            tokens = slice(b * P, (b + 1) * P)
+            entries = slice(b * P // 16, (b + 1) * P // 16)
+            dh = ps.tile([P, H], F32, name="bank_dh", tag="bank")
+            plain = held([P, ROWS, P], F32, f"plain{b}", f"da_turned{b - 2}" if b >= 2 else None)
+            second = held([P, ROWS, P], F32, f"second{b}", f"neg_slope{b - 2}" if b >= 2 else None)
+            first = held([P, ROWS, P], F32, f"first{b}")
+            for j in range(ROWS):
+                nc.scalar.activation(plain[:, j, :], y[j][:].indirect(pos_t[0][:, entries]), ACT.Copy)
+                nc.vector.tensor_tensor(
+                    second[:, j, :], y[j][:].indirect(pos_t[1][:, entries]), gate_t[:, 1, tokens], ALU.mult
+                )
+                nc.tensor.matmul(
+                    dh[:, j * P : (j + 1) * P], second[:, j, :], ident[:],
+                    start=(j == 0), stop=False, is_transpose=True,
+                )
+            nc.vector.tensor_tensor(first[:], plain[:], gate_t[:, 0:1, tokens].to_broadcast([P, ROWS, P]), ALU.mult)
+            for j in range(ROWS):
+                nc.tensor.matmul(
+                    dh[:, j * P : (j + 1) * P], first[:, j, :], ident[:],
+                    start=False, stop=(j == ROWS - 1), is_transpose=True,
+                )
+            return dh
+
+        def finish(b, dh):
+            tokens = slice(b * P, (b + 1) * P)
+            da_turned = held([P, H], BF16, f"da_turned{b}")
+            nc.vector.scalar_tensor_tensor(da_turned[:], dh[:], -1.0, neg_slope[b][:], ALU.mult, ALU.mult)
+            pairs = da_turned[:].bitcast(F32)
+            back = ps.tile([P, 2, P], F32, name="bank_back", tag="bank")
+            for u in range(2):
+                nc.tensor.transpose(back[:, u, :], pairs[:, u : H // 2 : 2], ident[:])
+            da = held([P, 4 * P], BF16, f"da{b}")
+            nc.scalar.copy(
+                da[:].bitcast(F32).rearrange("p (t u) -> p t u", u=2), back[:].rearrange("p u t -> p t u")
+            )
+            da_w = held([P, P], U32, f"da_w{b}")
+            da_sc = held([P, P], U8, f"da_sc{b}")
+            nc.vector.quantize_mx(out=da_w[:].bitcast(FP8X4), scales=da_sc[:], in_=da[:])
+            res = ps.tile([P, 4, P], F32, name="bank_res", tag="bank")
+            for j in range(4):
+                nc.tensor.matmul_mx(
+                    out=res[:, j, :],
+                    lhsT=w1_w[:, 2 * j * P : 2 * (j + 1) * P].bitcast(FP4X4),
+                    lhsT_scale=w1_sc[:, j * P : (j + 1) * P],
+                    rhs=da_w[:].bitcast(FP8X4),
+                    rhs_scale=da_sc[:],
+                    start=True,
+                    stop=True,
+                )
+            rounded = held([P, 4 * P], BF16, f"rounded{b}")
+            nc.scalar.copy(rounded[:].rearrange("p (t j) -> p t j", j=4), res[:].rearrange("p j t -> p t j"))
+            exact = held([P, 4, P], F32, f"exact{b}")
+            nc.scalar.copy(exact[:], res[:])
+            nc.sync.dma_start(out_rows[:, :, tokens], exact[:])
+            nc.vector.quantize_mx(
+                out=out_codes[:, tokens].bitcast(FP8X4), scales=out_sc[:, tokens], in_=rounded[:]
+            )
+            nc.sync.dma_start(out_words[:, tokens], out_codes[:, tokens].bitcast(I32))
+
+        dh = [combine(0)]
+        w1_w = held([P, 2 * K], U8, "w1_w", "second0")
+        w1_sc = held([P, K], U8, "w1_sc", "plain0")
+        nc.vector.tensor_copy(
+            w1_w[:].bitcast(U16).rearrange("p (j m) -> p j m", j=4),
+            w1_raw[:].bitcast(U16).rearrange("p (m j) -> p j m", j=4),
+        )
+        nc.vector.tensor_copy(
+            w1_sc[:].rearrange("p (j m) -> p m j", j=4), w1_sc_raw[:].rearrange("p (m j) -> p m j", j=4)
+        )
+
+        for b in range(1, BLOCKS):
+            dh.append(combine(b))
+            finish(b - 1, dh[b - 1])
+        finish(BLOCKS - 1, dh[BLOCKS - 1])
+
+        out_sc_rows = out_2[0].rearrange("(q r) t -> r q t", r=4)
+        for r in range(4):
+            queue = nc.sync if r % 2 == 0 else nc.scalar
+            queue.dma_start(out_sc_rows[r].bitcast(I32), out_sc[r:P:32, :].bitcast(I32))

@@ -39,10 +39,11 @@ def tile_moe_sub_silu_kernel(
         pos_t = [sb.tile([P, T // 16], U16, name=f"pos_t{r}") for r in range(2)]
 
         dy_sc = held([P, T], U8, "dy_sc")
-        w2_sc = held([P, E * PASSES, H], U8, "w2_sc")
+        w2_sc = [held([P, 2 * PASSES, H], U8, f"w2_sc{g}") for g in range(2)]
         w1_sc_raw = held([P, K], U8, "w1_sc_raw")
         nc.vector.memset(dy_sc[:].bitcast(I32), 0)
-        nc.vector.memset(w2_sc[:].bitcast(I32), 0)
+        for g in range(2):
+            nc.vector.memset(w2_sc[g][:].bitcast(I32), 0)
         nc.vector.memset(w1_sc_raw[:].bitcast(I32), 0)
 
         dy_w = held([P, PASSES, T], U32, "dy_w")
@@ -60,13 +61,14 @@ def tile_moe_sub_silu_kernel(
             )
         for h in range(2):
             nc.sync.dma_start(a_t[h][:], a_rows[:, 2 * h : 2 * h + 2, :])
-        w2_sc_rows = w2t_scales.rearrange("e s (q r) i -> r q (e s) i", r=4)
-        for r in range(4):
-            nc.sync.dma_start(w2_sc[r:P:32, :, :].bitcast(I32), w2_sc_rows[r].bitcast(I32))
-        for e in range(E):
-            nc.sync.dma_start(
-                w2_w[e][:].bitcast(I32), w2t_words[e].rearrange("s p i d -> p s (i d)").bitcast(I32)
-            )
+        w2_sc_rows = w2t_scales.rearrange("(g e) s (q r) i -> g r q (e s) i", e=2, r=4)
+        for g in range(2):
+            for r in range(4):
+                nc.sync.dma_start(w2_sc[g][8 * g + r : P : 32, :, :].bitcast(I32), w2_sc_rows[g, r].bitcast(I32))
+            for e in (2 * g, 2 * g + 1):
+                nc.sync.dma_start(
+                    w2_w[e][:].bitcast(I32), w2t_words[e].rearrange("s p i d -> p s (i d)").bitcast(I32)
+                )
         nc.sync.dma_start(pos_t[0][:], pos1)
         nc.sync.dma_start(pos_t[1][:], pos2)
         nc.sync.dma_start(gate_t[:], gate.rearrange("r p t -> p r t"))
@@ -88,7 +90,10 @@ def tile_moe_sub_silu_kernel(
             nc.scalar.activation(silu_neg[:, :, j * P : (j + 1) * P], bank[:], ACT.Silu, scale=-1.0)
             a_turned.append(bank)
 
-        y = [held([P, E * C], F32, f"y{j}") for j in range(ROWS)]
+        one_less = held([P, BLOCKS, H], F32, "one_less")
+        nc.gpsimd.tensor_scalar(one_less[:], silu_neg[:], -1.0, 1.0, ALU.mult, ALU.add)
+
+        y = [held([P, 2 * E * C], F32, f"y{half}") for half in range(ROWS // 2)]
 
         def slots(e):
             return offs_t[:, e * C // 16 : (e + 1) * C // 16]
@@ -108,26 +113,23 @@ def tile_moe_sub_silu_kernel(
                         nc.tensor.matmul_mx(
                             out=bank[:, jj, :],
                             lhsT=w2_w[e][:, s, cols].bitcast(FP8X4),
-                            lhsT_scale=w2_sc[:, e * PASSES + s, cols],
+                            lhsT_scale=w2_sc[e // 2][8 * (e // 2) :, (e % 2) * PASSES + s, cols],
                             rhs=g_w[e][s][:].bitcast(FP8X4),
                             rhs_scale=g_sc[4 * s :, :],
                             start=(s == 0),
                             stop=(s == PASSES - 1),
                         )
-                for jj in range(2):
-                    leave = nc.vector.tensor_copy if (e, half) == (E - 1, 1) else nc.scalar.copy
-                    leave(y[2 * half + jj][:, e * C : (e + 1) * C], bank[:, jj, :])
+                leave = nc.vector.tensor_copy if half == 1 and e >= E - 2 else nc.scalar.copy
+                leave(y[half][:].rearrange("p (j c) -> p j c", j=2)[:, :, e * C : (e + 1) * C], bank[:])
 
         for j in range(ROWS):
             nc.scalar.activation(sig[:, :, j * P : (j + 1) * P], a_turned[j][:], ACT.Sigmoid)
         for e in range(E - 1):
             expert(e)
 
-        neg_slope = [held([P, H], F32, f"neg_slope{b}") for b in range(BLOCKS)]
+        slope = [held([P, H], F32, f"slope{b}") for b in range(BLOCKS)]
         for b in range(BLOCKS):
-            nc.vector.scalar_tensor_tensor(
-                neg_slope[b][:], silu_neg[:, b, :], 1.0, sig[:, b, :], ALU.subtract, ALU.mult
-            )
+            nc.gpsimd.tensor_tensor(slope[b][:], one_less[:, b, :], sig[:, b, :], ALU.mult)
 
         expert(E - 1)
 
@@ -140,30 +142,36 @@ def tile_moe_sub_silu_kernel(
             tokens = slice(b * P, (b + 1) * P)
             entries = slice(b * P // 16, (b + 1) * P // 16)
             dh = ps.tile([P, H], F32, name="bank_dh", tag="bank")
-            plain = held([P, ROWS, P], F32, f"plain{b}", f"da_turned{b - 2}" if b >= 2 else None)
-            second = held([P, ROWS, P], F32, f"second{b}", f"neg_slope{b - 2}" if b >= 2 else None)
-            first = held([P, ROWS, P], F32, f"first{b}")
-            for j in range(ROWS):
-                nc.scalar.activation(plain[:, j, :], y[j][:].indirect(pos_t[0][:, entries]), ACT.Copy)
-                nc.vector.tensor_tensor(
-                    second[:, j, :], y[j][:].indirect(pos_t[1][:, entries]), gate_t[:, 1, tokens], ALU.mult
-                )
-                nc.tensor.matmul(
-                    dh[:, j * P : (j + 1) * P], second[:, j, :], ident[:],
-                    start=(j == 0), stop=False, is_transpose=True,
-                )
-            nc.vector.tensor_tensor(first[:], plain[:], gate_t[:, 0:1, tokens].to_broadcast([P, ROWS, P]), ALU.mult)
-            for j in range(ROWS):
-                nc.tensor.matmul(
-                    dh[:, j * P : (j + 1) * P], first[:, j, :], ident[:],
-                    start=False, stop=(j == ROWS - 1), is_transpose=True,
-                )
+            plain = held([P, 2, 2, P], F32, f"plain{b}", f"da_turned{b - 2}" if b >= 2 else None)
+            fused = held([P, 2, 2, P], F32, f"fused{b}", f"slope{b - 2}" if b >= 2 else None)
+            gated = held([P, 2, 2, P], F32, f"gated{b}")
+            for half in range(2):
+                for r in range(2):
+                    nc.scalar.activation(
+                        plain[:, half, r, :], y[half][:, E * C :].indirect(pos_t[r][:, entries]), ACT.Copy
+                    )
+                    nc.vector.tensor_tensor(
+                        fused[:, half, r, :], y[half][:].indirect(pos_t[r][:, entries]), gate_t[:, r, tokens], ALU.mult
+                    )
+                    nc.tensor.matmul(
+                        dh[:, 2 * half * P : (2 * half + 1) * P], fused[:, half, r, :], ident[:],
+                        start=(half == 0 and r == 0), stop=False, is_transpose=True,
+                    )
+            nc.vector.tensor_tensor(
+                gated[:], plain[:], gate_t[:, :, tokens].unsqueeze(1).to_broadcast([P, 2, 2, P]), ALU.mult
+            )
+            for half in range(2):
+                for r in range(2):
+                    nc.tensor.matmul(
+                        dh[:, (2 * half + 1) * P : (2 * half + 2) * P], gated[:, half, r, :], ident[:],
+                        start=False, stop=(half == 1 and r == 1), is_transpose=True,
+                    )
             return dh
 
         def finish(b, dh):
             tokens = slice(b * P, (b + 1) * P)
             da_turned = held([P, H], BF16, f"da_turned{b}")
-            nc.vector.scalar_tensor_tensor(da_turned[:], dh[:], -1.0, neg_slope[b][:], ALU.mult, ALU.mult)
+            nc.vector.tensor_tensor(da_turned[:], dh[:], slope[b][:], ALU.mult)
             pairs = da_turned[:].bitcast(F32)
             back = ps.tile([P, 2, P], F32, name="bank_back", tag="bank")
             for u in range(2):
@@ -187,9 +195,16 @@ def tile_moe_sub_silu_kernel(
                     stop=True,
                 )
             rounded = held([P, 4 * P], BF16, f"rounded{b}")
-            nc.scalar.copy(rounded[:].rearrange("p (t j) -> p t j", j=4), res[:].rearrange("p j t -> p t j"))
             exact = held([P, 4, P], F32, f"exact{b}")
-            nc.scalar.copy(exact[:], res[:])
+            if b < BLOCKS - 1:
+                nc.scalar.copy(rounded[:].rearrange("p (t j) -> p t j", j=4), res[:].rearrange("p j t -> p t j"))
+                nc.scalar.copy(exact[:], res[:])
+            else:
+                nc.scalar.copy(exact[:], res[:])
+                nc.vector.tensor_copy(
+                    rounded[:].rearrange("p (c i j) -> p c j i", i=4, j=4),
+                    exact[:].rearrange("p j (c i) -> p c j i", i=4),
+                )
             nc.sync.dma_start(out_rows[:, :, tokens], exact[:])
             nc.vector.quantize_mx(
                 out=out_codes[:, tokens].bitcast(FP8X4), scales=out_sc[:, tokens], in_=rounded[:]
@@ -197,7 +212,7 @@ def tile_moe_sub_silu_kernel(
             nc.sync.dma_start(out_words[:, tokens], out_codes[:, tokens].bitcast(I32))
 
         dh = [combine(0)]
-        w1_w = held([P, 2 * K], U8, "w1_w", "second0")
+        w1_w = held([P, 2 * K], U8, "w1_w", "fused0")
         w1_sc = held([P, K], U8, "w1_sc", "plain0")
         nc.vector.tensor_copy(
             w1_w[:].bitcast(U16).rearrange("p (j m) -> p j m", j=4),

@@ -62,16 +62,15 @@ def tile_moe_sub_silu_kernel(
         for h in range(2):
             nc.sync.dma_start(a_t[h][:], a_rows[:, 2 * h : 2 * h + 2, :])
         w2_sc_rows = w2t_scales.rearrange("(g e) s (q r) i -> g r q (e s) i", e=2, r=4)
-        for g in range(2):
-            for r in range(4):
-                nc.sync.dma_start(w2_sc[g][8 * g + r : P : 32, :, :].bitcast(I32), w2_sc_rows[g, r].bitcast(I32))
-            for e in (2 * g, 2 * g + 1):
-                nc.sync.dma_start(
-                    w2_w[e][:].bitcast(I32), w2t_words[e].rearrange("s p i d -> p s (i d)").bitcast(I32)
-                )
+        for e in range(E):
+            nc.sync.dma_start(w2_w[e][:].bitcast(I32), w2t_words[e].rearrange("s p i d -> p s (i d)").bitcast(I32))
+            if e % 2 == 0:
+                g = e // 2
+                for r in range(4):
+                    nc.sync.dma_start(w2_sc[g][8 * g + r : P : 32, :, :].bitcast(I32), w2_sc_rows[g, r].bitcast(I32))
+        nc.sync.dma_start(gate_t[:], gate.rearrange("r p t -> p r t"))
         nc.sync.dma_start(pos_t[0][:], pos1)
         nc.sync.dma_start(pos_t[1][:], pos2)
-        nc.sync.dma_start(gate_t[:], gate.rearrange("r p t -> p r t"))
         nc.sync.dma_start(w1_raw[:].bitcast(I32), w1t_words[0].bitcast(I32))
         w1_sc_rows = w1t_scales[0].rearrange("(q r) k -> r q k", r=4)
         for r in range(4):
@@ -131,6 +130,16 @@ def tile_moe_sub_silu_kernel(
         for b in range(BLOCKS):
             nc.gpsimd.tensor_tensor(slope[b][:], one_less[:, b, :], sig[:, b, :], ALU.mult)
 
+        w1_w = held([P, 2 * K], U8, "w1_w")
+        w1_sc = held([P, K], U8, "w1_sc")
+        nc.vector.tensor_copy(
+            w1_w[:].bitcast(U16).rearrange("p (j m) -> p j m", j=4),
+            w1_raw[:].bitcast(U16).rearrange("p (m j) -> p j m", j=4),
+        )
+        nc.vector.tensor_copy(
+            w1_sc[:].rearrange("p (j m) -> p m j", j=4), w1_sc_raw[:].rearrange("p (m j) -> p m j", j=4)
+        )
+
         expert(E - 1)
 
         out_codes = held([P, T], U32, "out_codes")
@@ -138,20 +147,22 @@ def tile_moe_sub_silu_kernel(
         out_rows = out_0.rearrange("(p j) t -> p j t", j=4)
         out_words = out_1[0].rearrange("p t d -> p (t d)").bitcast(I32)
 
+        def picked(window, r, b):
+            return window.indirect(pos_t[r][:, b * P // 16 : (b + 1) * P // 16])
+
         def combine(b):
             tokens = slice(b * P, (b + 1) * P)
-            entries = slice(b * P // 16, (b + 1) * P // 16)
             dh = ps.tile([P, H], F32, name="bank_dh", tag="bank")
-            plain = held([P, 2, 2, P], F32, f"plain{b}", f"da_turned{b - 2}" if b >= 2 else None)
-            fused = held([P, 2, 2, P], F32, f"fused{b}", f"slope{b - 2}" if b >= 2 else None)
+            plain = held([P, 2, 2, P], F32, f"plain{b}")
+            fused = held([P, 2, 2, P], F32, f"fused{b}")
             gated = held([P, 2, 2, P], F32, f"gated{b}")
             for half in range(2):
                 for r in range(2):
-                    nc.scalar.activation(
-                        plain[:, half, r, :], y[half][:, E * C :].indirect(pos_t[r][:, entries]), ACT.Copy
-                    )
+                    nc.scalar.activation(plain[:, half, r, :], picked(y[half][:, E * C :], r, b), ACT.Copy)
+            for half in range(2):
+                for r in range(2):
                     nc.vector.tensor_tensor(
-                        fused[:, half, r, :], y[half][:].indirect(pos_t[r][:, entries]), gate_t[:, r, tokens], ALU.mult
+                        fused[:, half, r, :], picked(y[half][:], r, b), gate_t[:, r, tokens], ALU.mult
                     )
                     nc.tensor.matmul(
                         dh[:, 2 * half * P : (2 * half + 1) * P], fused[:, half, r, :], ident[:],
@@ -196,36 +207,20 @@ def tile_moe_sub_silu_kernel(
                 )
             rounded = held([P, 4 * P], BF16, f"rounded{b}")
             exact = held([P, 4, P], F32, f"exact{b}")
-            if b < BLOCKS - 1:
-                nc.scalar.copy(rounded[:].rearrange("p (t j) -> p t j", j=4), res[:].rearrange("p j t -> p t j"))
-                nc.scalar.copy(exact[:], res[:])
-            else:
-                nc.scalar.copy(exact[:], res[:])
-                nc.vector.tensor_copy(
-                    rounded[:].rearrange("p (c i j) -> p c j i", i=4, j=4),
-                    exact[:].rearrange("p j (c i) -> p c j i", i=4),
-                )
+            nc.scalar.copy(exact[:], res[:])
+            nc.vector.tensor_copy(
+                rounded[:].rearrange("p (c i j) -> p c j i", i=4, j=4),
+                exact[:].rearrange("p j (c i) -> p c j i", i=4),
+            )
             nc.sync.dma_start(out_rows[:, :, tokens], exact[:])
             nc.vector.quantize_mx(
                 out=out_codes[:, tokens].bitcast(FP8X4), scales=out_sc[:, tokens], in_=rounded[:]
             )
             nc.sync.dma_start(out_words[:, tokens], out_codes[:, tokens].bitcast(I32))
 
-        dh = [combine(0)]
-        w1_w = held([P, 2 * K], U8, "w1_w", "fused0")
-        w1_sc = held([P, K], U8, "w1_sc", "plain0")
-        nc.vector.tensor_copy(
-            w1_w[:].bitcast(U16).rearrange("p (j m) -> p j m", j=4),
-            w1_raw[:].bitcast(U16).rearrange("p (m j) -> p j m", j=4),
-        )
-        nc.vector.tensor_copy(
-            w1_sc[:].rearrange("p (j m) -> p m j", j=4), w1_sc_raw[:].rearrange("p (m j) -> p m j", j=4)
-        )
-
-        for b in range(1, BLOCKS):
-            dh.append(combine(b))
-            finish(b - 1, dh[b - 1])
-        finish(BLOCKS - 1, dh[BLOCKS - 1])
+        sums = [combine(b) for b in range(BLOCKS)]
+        for b in range(BLOCKS):
+            finish(b, sums[b])
 
         out_sc_rows = out_2[0].rearrange("(q r) t -> r q t", r=4)
         for r in range(4):

@@ -18,9 +18,15 @@ ALU = mybir.AluOpType
 ACT = mybir.ActivationFunctionType
 
 P = 128
-PASSES = N // 512
+PACK = 4
+PASSES = N // (P * PACK)
 ROWS = H // P
+HALVES = ROWS // 2
 BLOCKS = T // P
+SLOTS = E * C
+PER_COLUMN = 16
+BANKS = 8
+GROUP_ROW = 8
 
 
 def tile_moe_sub_silu_kernel(
@@ -30,24 +36,24 @@ def tile_moe_sub_silu_kernel(
     nc = tc.nc
     with ExitStack() as ctx:
         sb = ctx.enter_context(tc.tile_pool(name="sb", bufs=1))
-        ps = ctx.enter_context(tc.psum_pool(name="ps", bufs=8))
+        ps = ctx.enter_context(tc.psum_pool(name="ps", bufs=BANKS))
 
         def held(shape, dtype, name, tag=None):
             return sb.tile(shape, dtype, name=name, tag=tag or name, align_bytes=64)
 
-        offs_t = sb.tile([P, E * C // 16], U16, name="offs_t")
-        pos_t = [sb.tile([P, T // 16], U16, name=f"pos_t{r}") for r in range(2)]
+        offs_t = sb.tile([P, SLOTS // PER_COLUMN], U16, name="offs_t")
+        pos_t = [sb.tile([P, T // PER_COLUMN], U16, name=f"pos_t{r}") for r in range(2)]
 
         dy_sc = held([P, T], U8, "dy_sc")
-        w2_sc = [held([P, 2 * PASSES, H], U8, f"w2_sc{g}") for g in range(2)]
+        w2_sc = [held([P, 2 * PASSES, H], U8, f"w2_sc{g}") for g in range(E // 2)]
         w1_sc_raw = held([P, K], U8, "w1_sc_raw")
         nc.vector.memset(dy_sc[:].bitcast(I32), 0)
-        for g in range(2):
+        for g in range(E // 2):
             nc.vector.memset(w2_sc[g][:].bitcast(I32), 0)
         nc.vector.memset(w1_sc_raw[:].bitcast(I32), 0)
 
         dy_w = held([P, PASSES, T], U32, "dy_w")
-        a_t = [held([P, 2, T], F32, f"a_t{h}") for h in range(2)]
+        a_t = [held([P, 2, T], F32, f"a_t{half}") for half in range(HALVES)]
         w2_w = [held([P, PASSES, H], U32, f"w2_w{e}") for e in range(E)]
         gate_t = held([P, 2, T], F32, "gate_t")
         w1_raw = held([P, 2 * K], U8, "w1_raw")
@@ -55,26 +61,29 @@ def tile_moe_sub_silu_kernel(
         nc.sync.dma_start(offs_t[:], offs)
         a_rows = a.rearrange("(j p) t -> p j t", p=P)
         nc.sync.dma_start(dy_w[:].bitcast(I32), dy_words.rearrange("s p t d -> p s (t d)").bitcast(I32))
-        for q in range(4):
+        for quad in range(P // 32):
             nc.scalar.dma_start(
-                dy_sc[32 * q : 32 * q + 4 * PASSES, :].bitcast(I32), dy_scales[:, 4 * q : 4 * q + 4, :].bitcast(I32)
+                dy_sc[32 * quad : 32 * quad + PACK * PASSES, :].bitcast(I32),
+                dy_scales[:, PACK * quad : PACK * (quad + 1), :].bitcast(I32),
             )
-        for h in range(2):
-            nc.sync.dma_start(a_t[h][:], a_rows[:, 2 * h : 2 * h + 2, :])
-        w2_sc_rows = w2t_scales.rearrange("(g e) s (q r) i -> g r q (e s) i", e=2, r=4)
+        for half in range(HALVES):
+            nc.sync.dma_start(a_t[half][:], a_rows[:, 2 * half : 2 * half + 2, :])
+        w2_sc_rows = w2t_scales.rearrange("(g e) s (q r) i -> g r q (e s) i", e=2, r=PACK)
         for e in range(E):
             nc.sync.dma_start(w2_w[e][:].bitcast(I32), w2t_words[e].rearrange("s p i d -> p s (i d)").bitcast(I32))
             if e % 2 == 0:
                 g = e // 2
-                for r in range(4):
-                    nc.sync.dma_start(w2_sc[g][8 * g + r : P : 32, :, :].bitcast(I32), w2_sc_rows[g, r].bitcast(I32))
-        nc.sync.dma_start(gate_t[:], gate.rearrange("r p t -> p r t"))
+                for row in range(PACK):
+                    nc.sync.dma_start(
+                        w2_sc[g][GROUP_ROW * g + row : P : 32, :, :].bitcast(I32), w2_sc_rows[g, row].bitcast(I32)
+                    )
+        nc.sync.dma_start(w1_raw[:].bitcast(I32), w1t_words[0].bitcast(I32))
+        w1_sc_rows = w1t_scales[0].rearrange("(q r) k -> r q k", r=PACK)
+        for row in range(PACK):
+            nc.sync.dma_start(w1_sc_raw[row:P:32, :].bitcast(I32), w1_sc_rows[row].bitcast(I32))
         nc.sync.dma_start(pos_t[0][:], pos1)
         nc.sync.dma_start(pos_t[1][:], pos2)
-        nc.sync.dma_start(w1_raw[:].bitcast(I32), w1t_words[0].bitcast(I32))
-        w1_sc_rows = w1t_scales[0].rearrange("(q r) k -> r q k", r=4)
-        for r in range(4):
-            nc.sync.dma_start(w1_sc_raw[r:P:32, :].bitcast(I32), w1_sc_rows[r].bitcast(I32))
+        nc.sync.dma_start(gate_t[:], gate.rearrange("r p t -> p r t"))
 
         ident = held([P, P], F32, "ident")
         make_identity(nc, ident[:])
@@ -83,43 +92,40 @@ def tile_moe_sub_silu_kernel(
         sig = held([P, BLOCKS, H], F32, "sig")
         a_turned = []
         for j in range(ROWS):
-            bank = ps.tile([P, BLOCKS, P], F32, name="bank_a", tag="bank")
+            bank_a = ps.tile([P, BLOCKS, P], F32, name="bank_a", tag="bank")
             for b in range(BLOCKS):
-                nc.tensor.transpose(bank[:, b, :], a_t[j // 2][:, j % 2, b * P : (b + 1) * P], ident[:])
-            nc.scalar.activation(silu_neg[:, :, j * P : (j + 1) * P], bank[:], ACT.Silu, scale=-1.0)
-            a_turned.append(bank)
+                nc.tensor.transpose(bank_a[:, b, :], a_t[j // 2][:, j % 2, b * P : (b + 1) * P], ident[:])
+            nc.scalar.activation(silu_neg[:, :, j * P : (j + 1) * P], bank_a[:], ACT.Silu, scale=-1.0)
+            a_turned.append(bank_a)
 
         one_less = held([P, BLOCKS, H], F32, "one_less")
         nc.gpsimd.tensor_scalar(one_less[:], silu_neg[:], -1.0, 1.0, ALU.mult, ALU.add)
 
-        y = [held([P, 2 * E * C], F32, f"y{half}") for half in range(ROWS // 2)]
-
-        def slots(e):
-            return offs_t[:, e * C // 16 : (e + 1) * C // 16]
-
+        y = [held([P, 2 * SLOTS], F32, f"y{half}") for half in range(HALVES)]
         g_w = [[held([P, C], U32, f"g_w{e}_{s}") for s in range(PASSES)] for e in range(E)]
 
         def expert(e):
+            slots = offs_t[:, e * C // PER_COLUMN : (e + 1) * C // PER_COLUMN]
             g_sc = held([P, C], U8, f"g_sc{e}")
-            nc.vector.tensor_copy(g_sc[:], dy_sc[:].indirect(slots(e)))
+            nc.vector.tensor_copy(g_sc[:], dy_sc[:].indirect(slots))
             for s in range(PASSES):
-                nc.vector.tensor_copy(g_w[e][s][:], dy_w[:, s, :].indirect(slots(e)))
-            for half in range(ROWS // 2):
-                bank = ps.tile([P, 2, C], F32, name="bank_y", tag="bank")
-                for jj in range(2):
-                    cols = slice((2 * half + jj) * P, (2 * half + jj + 1) * P)
+                nc.vector.tensor_copy(g_w[e][s][:], dy_w[:, s, :].indirect(slots))
+            for half in range(HALVES):
+                bank_y = ps.tile([P, 2, C], F32, name="bank_y", tag="bank")
+                for odd in range(2):
+                    cols = slice((2 * half + odd) * P, (2 * half + odd + 1) * P)
                     for s in range(PASSES):
                         nc.tensor.matmul_mx(
-                            out=bank[:, jj, :],
+                            out=bank_y[:, odd, :],
                             lhsT=w2_w[e][:, s, cols].bitcast(FP8X4),
-                            lhsT_scale=w2_sc[e // 2][8 * (e // 2) :, (e % 2) * PASSES + s, cols],
+                            lhsT_scale=w2_sc[e // 2][GROUP_ROW * (e // 2) :, (e % 2) * PASSES + s, cols],
                             rhs=g_w[e][s][:].bitcast(FP8X4),
-                            rhs_scale=g_sc[4 * s :, :],
+                            rhs_scale=g_sc[PACK * s :, :],
                             start=(s == 0),
                             stop=(s == PASSES - 1),
                         )
                 leave = nc.vector.tensor_copy if half == 1 and e >= E - 2 else nc.scalar.copy
-                leave(y[half][:].rearrange("p (j c) -> p j c", j=2)[:, :, e * C : (e + 1) * C], bank[:])
+                leave(y[half][:].rearrange("p (j c) -> p j c", j=2)[:, :, e * C : (e + 1) * C], bank_y[:])
 
         for j in range(ROWS):
             nc.scalar.activation(sig[:, :, j * P : (j + 1) * P], a_turned[j][:], ACT.Sigmoid)
@@ -133,33 +139,33 @@ def tile_moe_sub_silu_kernel(
         w1_w = held([P, 2 * K], U8, "w1_w")
         w1_sc = held([P, K], U8, "w1_sc")
         nc.vector.tensor_copy(
-            w1_w[:].bitcast(U16).rearrange("p (j m) -> p j m", j=4),
-            w1_raw[:].bitcast(U16).rearrange("p (m j) -> p j m", j=4),
+            w1_w[:].bitcast(U16).rearrange("p (j m) -> p j m", j=PACK),
+            w1_raw[:].bitcast(U16).rearrange("p (m j) -> p j m", j=PACK),
         )
         nc.vector.tensor_copy(
-            w1_sc[:].rearrange("p (j m) -> p m j", j=4), w1_sc_raw[:].rearrange("p (m j) -> p m j", j=4)
+            w1_sc[:].rearrange("p (j m) -> p m j", j=PACK), w1_sc_raw[:].rearrange("p (m j) -> p m j", j=PACK)
         )
 
         expert(E - 1)
 
         out_codes = held([P, T], U32, "out_codes")
         out_sc = held([P, T], U8, "out_sc")
-        out_rows = out_0.rearrange("(p j) t -> p j t", j=4)
+        out_rows = out_0.rearrange("(p j) t -> p j t", j=PACK)
         out_words = out_1[0].rearrange("p t d -> p (t d)").bitcast(I32)
 
         def picked(window, r, b):
-            return window.indirect(pos_t[r][:, b * P // 16 : (b + 1) * P // 16])
+            return window.indirect(pos_t[r][:, b * P // PER_COLUMN : (b + 1) * P // PER_COLUMN])
 
         def combine(b):
             tokens = slice(b * P, (b + 1) * P)
             dh = ps.tile([P, H], F32, name="bank_dh", tag="bank")
-            plain = held([P, 2, 2, P], F32, f"plain{b}")
-            fused = held([P, 2, 2, P], F32, f"fused{b}")
-            gated = held([P, 2, 2, P], F32, f"gated{b}")
-            for half in range(2):
+            plain = held([P, HALVES, 2, P], F32, f"plain{b}")
+            fused = held([P, HALVES, 2, P], F32, f"fused{b}", f"plain{b - 2}" if b >= 2 else None)
+            gated = held([P, HALVES, 2, P], F32, f"gated{b}")
+            for half in range(HALVES):
                 for r in range(2):
-                    nc.scalar.activation(plain[:, half, r, :], picked(y[half][:, E * C :], r, b), ACT.Copy)
-            for half in range(2):
+                    nc.scalar.activation(plain[:, half, r, :], picked(y[half][:, SLOTS:], r, b), ACT.Copy)
+            for half in range(HALVES):
                 for r in range(2):
                     nc.vector.tensor_tensor(
                         fused[:, half, r, :], picked(y[half][:], r, b), gate_t[:, r, tokens], ALU.mult
@@ -169,33 +175,35 @@ def tile_moe_sub_silu_kernel(
                         start=(half == 0 and r == 0), stop=False, is_transpose=True,
                     )
             nc.vector.tensor_tensor(
-                gated[:], plain[:], gate_t[:, :, tokens].unsqueeze(1).to_broadcast([P, 2, 2, P]), ALU.mult
+                gated[:], plain[:], gate_t[:, :, tokens].unsqueeze(1).to_broadcast([P, HALVES, 2, P]), ALU.mult
             )
-            for half in range(2):
+            for half in range(HALVES):
                 for r in range(2):
                     nc.tensor.matmul(
                         dh[:, (2 * half + 1) * P : (2 * half + 2) * P], gated[:, half, r, :], ident[:],
-                        start=False, stop=(half == 1 and r == 1), is_transpose=True,
+                        start=False, stop=(half == HALVES - 1 and r == 1), is_transpose=True,
                     )
             return dh
 
-        def finish(b, dh):
-            tokens = slice(b * P, (b + 1) * P)
-            da_turned = held([P, H], BF16, f"da_turned{b}")
+        def turn_back(b, dh):
+            da_turned = held([P, H], BF16, f"da_turned{b}", f"plain{b + 2}" if b < 2 else None)
             nc.vector.tensor_tensor(da_turned[:], dh[:], slope[b][:], ALU.mult)
             pairs = da_turned[:].bitcast(F32)
             back = ps.tile([P, 2, P], F32, name="bank_back", tag="bank")
             for u in range(2):
                 nc.tensor.transpose(back[:, u, :], pairs[:, u : H // 2 : 2], ident[:])
-            da = held([P, 4 * P], BF16, f"da{b}")
+            da = held([P, PACK * P], BF16, f"da{b}")
             nc.scalar.copy(
                 da[:].bitcast(F32).rearrange("p (t u) -> p t u", u=2), back[:].rearrange("p u t -> p t u")
             )
+            return da
+
+        def project(b, da):
             da_w = held([P, P], U32, f"da_w{b}")
             da_sc = held([P, P], U8, f"da_sc{b}")
             nc.vector.quantize_mx(out=da_w[:].bitcast(FP8X4), scales=da_sc[:], in_=da[:])
-            res = ps.tile([P, 4, P], F32, name="bank_res", tag="bank")
-            for j in range(4):
+            res = ps.tile([P, PACK, P], F32, name="bank_res", tag="bank")
+            for j in range(PACK):
                 nc.tensor.matmul_mx(
                     out=res[:, j, :],
                     lhsT=w1_w[:, 2 * j * P : 2 * (j + 1) * P].bitcast(FP4X4),
@@ -205,24 +213,31 @@ def tile_moe_sub_silu_kernel(
                     start=True,
                     stop=True,
                 )
-            rounded = held([P, 4 * P], BF16, f"rounded{b}")
-            exact = held([P, 4, P], F32, f"exact{b}")
+            exact = held([P, PACK, P], F32, f"exact{b}")
             nc.scalar.copy(exact[:], res[:])
+            nc.sync.dma_start(out_rows[:, :, b * P : (b + 1) * P], exact[:])
+            return exact
+
+        sums = [combine(b) for b in range(BLOCKS)]
+        grouped = [turn_back(b, sums[b]) for b in range(BLOCKS)]
+        results = [project(b, grouped[b]) for b in range(BLOCKS)]
+
+        rounded = [held([P, 2, PACK * P], BF16, f"rounded{pair}") for pair in range(BLOCKS // 2)]
+        for b in range(BLOCKS):
             nc.vector.tensor_copy(
-                rounded[:].rearrange("p (c i j) -> p c j i", i=4, j=4),
-                exact[:].rearrange("p j (c i) -> p c j i", i=4),
+                rounded[b // 2][:, b % 2, :].rearrange("p (c i j) -> p c j i", i=4, j=PACK),
+                results[b][:].rearrange("p j (c i) -> p c j i", i=4),
             )
-            nc.sync.dma_start(out_rows[:, :, tokens], exact[:])
+        for pair in range(BLOCKS // 2):
+            tokens = slice(2 * pair * P, 2 * (pair + 1) * P)
             nc.vector.quantize_mx(
-                out=out_codes[:, tokens].bitcast(FP8X4), scales=out_sc[:, tokens], in_=rounded[:]
+                out=out_codes[:, tokens].bitcast(FP8X4),
+                scales=out_sc[:, tokens],
+                in_=rounded[pair][:].rearrange("p b x -> p (b x)"),
             )
             nc.sync.dma_start(out_words[:, tokens], out_codes[:, tokens].bitcast(I32))
 
-        sums = [combine(b) for b in range(BLOCKS)]
-        for b in range(BLOCKS):
-            finish(b, sums[b])
-
-        out_sc_rows = out_2[0].rearrange("(q r) t -> r q t", r=4)
-        for r in range(4):
-            queue = nc.sync if r % 2 == 0 else nc.scalar
-            queue.dma_start(out_sc_rows[r].bitcast(I32), out_sc[r:P:32, :].bitcast(I32))
+        out_sc_rows = out_2[0].rearrange("(q r) t -> r q t", r=PACK)
+        for row in range(PACK):
+            queue = nc.sync if row % 2 == 0 else nc.scalar
+            queue.dma_start(out_sc_rows[row].bitcast(I32), out_sc[row:P:32, :].bitcast(I32))

from contextlib import ExitStack

import concourse.mybir as mybir
from concourse.masks import make_identity

K, T, E, C, H, N = 512, 512, 4, 256, 512, 1536
FLOPS = 2 * (E * C * N * H + H * K * T)

F32 = mybir.dt.float32
BF16 = mybir.dt.bfloat16
I32 = mybir.dt.int32
U32 = mybir.dt.uint32
U16 = mybir.dt.uint16
U8 = mybir.dt.uint8
FP8X4 = mybir.dt.float8_e4m3fn_x4
FP4X4 = mybir.dt.float4_e2m1fn_x4
ALU = mybir.AluOpType
ACT = mybir.ActivationFunctionType

P = 128
PACK = 4
PASSES = N // (P * PACK)
ROWS = H // P
HALVES = ROWS // 2
BLOCKS = T // P
SLOTS = E * C
PER_COLUMN = 16
BANKS = 8
GROUP_ROW = 8


def tile_moe_sub_silu_kernel(
    tc, dy_words, dy_scales, w2t_words, w2t_scales, w1t_words, w1t_scales, a, gate, offs, pos1, pos2,
    out_0, out_1, out_2,
):
    nc = tc.nc
    with ExitStack() as ctx:
        sb = ctx.enter_context(tc.tile_pool(name="sb", bufs=1))
        ps = ctx.enter_context(tc.psum_pool(name="ps", bufs=BANKS))

        def held(shape, dtype, name, tag=None):
            return sb.tile(shape, dtype, name=name, tag=tag or name, align_bytes=64)

        offs_t = sb.tile([P, SLOTS // PER_COLUMN], U16, name="offs_t")
        pos_t = [sb.tile([P, T // PER_COLUMN], U16, name=f"pos_t{r}") for r in range(2)]

        dy_sc = held([P, T], U8, "dy_sc")
        w2_sc = [held([P, 2 * PASSES, H], U8, f"w2_sc{g}") for g in range(E // 2)]
        w1_sc_raw = held([P, K], U8, "w1_sc_raw")
        nc.vector.memset(dy_sc[:].bitcast(I32), 0)
        for g in range(E // 2):
            nc.vector.memset(w2_sc[g][:].bitcast(I32), 0)
        nc.vector.memset(w1_sc_raw[:].bitcast(I32), 0)

        dy_w = held([P, PASSES, T], U32, "dy_w")
        a_t = [held([P, 2, T], F32, f"a_t{half}") for half in range(HALVES)]
        w2_w = [held([P, PASSES, H], U32, f"w2_w{e}") for e in range(E)]
        gate_t = held([P, 2, T], F32, "gate_t")
        w1_raw = held([P, 2 * K], U8, "w1_raw")

        nc.sync.dma_start(offs_t[:], offs)
        a_rows = a.rearrange("(j p) t -> p j t", p=P)
        nc.sync.dma_start(dy_w[:].bitcast(I32), dy_words.rearrange("s p t d -> p s (t d)").bitcast(I32))
        for quad in range(P // 32):
            nc.scalar.dma_start(
                dy_sc[32 * quad : 32 * quad + PACK * PASSES, :].bitcast(I32),
                dy_scales[:, PACK * quad : PACK * (quad + 1), :].bitcast(I32),
            )
        for half in range(HALVES):
            nc.sync.dma_start(a_t[half][:], a_rows[:, 2 * half : 2 * half + 2, :])
        w2_sc_rows = w2t_scales.rearrange("(g e) s (q r) i -> g r q (e s) i", e=2, r=PACK)
        for e in range(E):
            nc.sync.dma_start(w2_w[e][:].bitcast(I32), w2t_words[e].rearrange("s p i d -> p s (i d)").bitcast(I32))
            if e % 2 == 0:
                g = e // 2
                for row in range(PACK):
                    nc.sync.dma_start(
                        w2_sc[g][GROUP_ROW * g + row : P : 32, :, :].bitcast(I32), w2_sc_rows[g, row].bitcast(I32)
                    )
        nc.sync.dma_start(w1_raw[:].bitcast(I32), w1t_words[0].bitcast(I32))
        w1_sc_rows = w1t_scales[0].rearrange("(q r) k -> r q k", r=PACK)
        for row in range(PACK):
            nc.sync.dma_start(w1_sc_raw[row:P:32, :].bitcast(I32), w1_sc_rows[row].bitcast(I32))
        nc.sync.dma_start(pos_t[0][:], pos1)
        nc.sync.dma_start(pos_t[1][:], pos2)
        nc.sync.dma_start(gate_t[:], gate.rearrange("r p t -> p r t"))

        ident = held([P, P], F32, "ident")
        make_identity(nc, ident[:])

        silu_neg = held([P, BLOCKS, H], F32, "silu_neg")
        sig = held([P, BLOCKS, H], F32, "sig")
        a_turned = []
        for j in range(ROWS):
            bank_a = ps.tile([P, BLOCKS, P], F32, name="bank_a", tag="bank")
            for b in range(BLOCKS):
                nc.tensor.transpose(bank_a[:, b, :], a_t[j // 2][:, j % 2, b * P : (b + 1) * P], ident[:])
            nc.scalar.activation(silu_neg[:, :, j * P : (j + 1) * P], bank_a[:], ACT.Silu, scale=-1.0)
            a_turned.append(bank_a)

        one_less = held([P, BLOCKS, H], F32, "one_less")
        nc.gpsimd.tensor_scalar(one_less[:], silu_neg[:], -1.0, 1.0, ALU.mult, ALU.add)

        y = [held([P, 2 * SLOTS], F32, f"y{half}") for half in range(HALVES)]
        g_w = [[held([P, C], U32, f"g_w{e}_{s}") for s in range(PASSES)] for e in range(E)]

        def expert(e):
            slots = offs_t[:, e * C // PER_COLUMN : (e + 1) * C // PER_COLUMN]
            g_sc = held([P, C], U8, f"g_sc{e}")
            nc.vector.tensor_copy(g_sc[:], dy_sc[:].indirect(slots))
            for s in range(PASSES):
                nc.vector.tensor_copy(g_w[e][s][:], dy_w[:, s, :].indirect(slots))
            for half in range(HALVES):
                bank_y = ps.tile([P, 2, C], F32, name="bank_y", tag="bank")
                for odd in range(2):
                    cols = slice((2 * half + odd) * P, (2 * half + odd + 1) * P)
                    for s in range(PASSES):
                        nc.tensor.matmul_mx(
                            out=bank_y[:, odd, :],
                            lhsT=w2_w[e][:, s, cols].bitcast(FP8X4),
                            lhsT_scale=w2_sc[e // 2][GROUP_ROW * (e // 2) :, (e % 2) * PASSES + s, cols],
                            rhs=g_w[e][s][:].bitcast(FP8X4),
                            rhs_scale=g_sc[PACK * s :, :],
                            start=(s == 0),
                            stop=(s == PASSES - 1),
                        )
                leave = nc.vector.tensor_copy if half == 1 and e >= E - 2 else nc.scalar.copy
                leave(y[half][:].rearrange("p (j c) -> p j c", j=2)[:, :, e * C : (e + 1) * C], bank_y[:])

        for j in range(ROWS):
            nc.scalar.activation(sig[:, :, j * P : (j + 1) * P], a_turned[j][:], ACT.Sigmoid)
        for e in range(E - 1):
            expert(e)

        slope = [held([P, H], F32, f"slope{b}") for b in range(BLOCKS)]
        for b in range(BLOCKS):
            nc.gpsimd.tensor_tensor(slope[b][:], one_less[:, b, :], sig[:, b, :], ALU.mult)

        w1_w = held([P, 2 * K], U8, "w1_w")
        w1_sc = held([P, K], U8, "w1_sc")
        nc.vector.tensor_copy(
            w1_w[:].bitcast(U16).rearrange("p (j m) -> p j m", j=PACK),
            w1_raw[:].bitcast(U16).rearrange("p (m j) -> p j m", j=PACK),
        )
        nc.vector.tensor_copy(
            w1_sc[:].rearrange("p (j m) -> p m j", j=PACK), w1_sc_raw[:].rearrange("p (m j) -> p m j", j=PACK)
        )

        expert(E - 1)

        out_codes = held([P, T], U32, "out_codes")
        out_sc = held([P, T], U8, "out_sc")
        out_rows = out_0.rearrange("(p j) t -> p j t", j=PACK)
        out_words = out_1[0].rearrange("p t d -> p (t d)").bitcast(I32)

        def picked(window, r, b):
            return window.indirect(pos_t[r][:, b * P // PER_COLUMN : (b + 1) * P // PER_COLUMN])

        def combine(b):
            tokens = slice(b * P, (b + 1) * P)
            dh = ps.tile([P, H], F32, name="bank_dh", tag="bank")
            plain = held([P, HALVES, 2, P], F32, f"plain{b}")
            fused = held([P, HALVES, 2, P], F32, f"fused{b}", f"plain{b - 2}" if b >= 2 else None)
            gated = held([P, HALVES, 2, P], F32, f"gated{b}")
            for half in range(HALVES):
                for r in range(2):
                    nc.scalar.activation(plain[:, half, r, :], picked(y[half][:, SLOTS:], r, b), ACT.Copy)
            for half in range(HALVES):
                for r in range(2):
                    nc.vector.tensor_tensor(
                        fused[:, half, r, :], picked(y[half][:], r, b), gate_t[:, r, tokens], ALU.mult
                    )
                    nc.tensor.matmul(
                        dh[:, 2 * half * P : (2 * half + 1) * P], fused[:, half, r, :], ident[:],
                        start=(half == 0 and r == 0), stop=False, is_transpose=True,
                    )
            nc.vector.tensor_tensor(
                gated[:], plain[:], gate_t[:, :, tokens].unsqueeze(1).to_broadcast([P, HALVES, 2, P]), ALU.mult
            )
            for half in range(HALVES):
                for r in range(2):
                    nc.tensor.matmul(
                        dh[:, (2 * half + 1) * P : (2 * half + 2) * P], gated[:, half, r, :], ident[:],
                        start=False, stop=(half == HALVES - 1 and r == 1), is_transpose=True,
                    )
            return dh

        def turn_back(b, dh):
            da_turned = held([P, H], BF16, f"da_turned{b}", f"plain{b + 2}" if b < 2 else None)
            nc.vector.tensor_tensor(da_turned[:], dh[:], slope[b][:], ALU.mult)
            pairs = da_turned[:].bitcast(F32)
            back = ps.tile([P, 2, P], F32, name="bank_back", tag="bank")
            for u in range(2):
                nc.tensor.transpose(back[:, u, :], pairs[:, u : H // 2 : 2], ident[:])
            da = held([P, PACK * P], BF16, f"da{b}")
            nc.scalar.copy(
                da[:].bitcast(F32).rearrange("p (t u) -> p t u", u=2), back[:].rearrange("p u t -> p t u")
            )
            return da

        def project(b, da):
            da_w = held([P, P], U32, f"da_w{b}")
            da_sc = held([P, P], U8, f"da_sc{b}")
            nc.vector.quantize_mx(out=da_w[:].bitcast(FP8X4), scales=da_sc[:], in_=da[:])
            res = ps.tile([P, PACK, P], F32, name="bank_res", tag="bank")
            for j in range(PACK):
                nc.tensor.matmul_mx(
                    out=res[:, j, :],
                    lhsT=w1_w[:, 2 * j * P : 2 * (j + 1) * P].bitcast(FP4X4),
                    lhsT_scale=w1_sc[:, j * P : (j + 1) * P],
                    rhs=da_w[:].bitcast(FP8X4),
                    rhs_scale=da_sc[:],
                    start=True,
                    stop=True,
                )
            exact = held([P, PACK, P], F32, f"exact{b}")
            nc.scalar.copy(exact[:], res[:])
            nc.sync.dma_start(out_rows[:, :, b * P : (b + 1) * P], exact[:])
            return exact

        sums = [combine(b) for b in range(BLOCKS)]
        grouped = [turn_back(b, sums[b]) for b in range(BLOCKS)]
        results = [project(b, grouped[b]) for b in range(BLOCKS)]

        rounded = [held([P, 2, PACK * P], BF16, f"rounded{pair}") for pair in range(BLOCKS // 2)]
        for b in range(BLOCKS):
            nc.vector.tensor_copy(
                rounded[b // 2][:, b % 2, :].rearrange("p (c i j) -> p c j i", i=4, j=PACK),
                results[b][:].rearrange("p j (c i) -> p c j i", i=4),
            )
        for pair in range(BLOCKS // 2):
            tokens = slice(2 * pair * P, 2 * (pair + 1) * P)
            nc.vector.quantize_mx(
                out=out_codes[:, tokens].bitcast(FP8X4),
                scales=out_sc[:, tokens],
                in_=rounded[pair][:].rearrange("p b x -> p (b x)"),
            )
            nc.sync.dma_start(out_words[:, tokens], out_codes[:, tokens].bitcast(I32))

        out_sc_rows = out_2[0].rearrange("(q r) t -> r q t", r=PACK)
        for row in range(PACK):
            queue = nc.sync if row % 2 == 0 else nc.scalar
            queue.dma_start(out_sc_rows[row].bitcast(I32), out_sc[row:P:32, :].bitcast(I32))
